import numpy as np
import ml_dtypes


def mxq(x, axis, fmt="e4m3"):
    dtype, down = {"e4m3": (ml_dtypes.float8_e4m3fn, 7), "e5m2": (ml_dtypes.float8_e5m2, 14)}[fmt]
    v = np.moveaxis(np.asarray(x, np.float32).astype(ml_dtypes.bfloat16).astype(np.float64), axis, -1)
    blocks = v.reshape(v.shape[:-1] + (-1, 32))
    amax = np.abs(blocks).max(-1, keepdims=True)
    byte = np.maximum(np.where(amax > 0, np.frexp(amax)[1] - 1 + 127, 0) - down, 1)
    scale = np.exp2(byte - 127.0)
    codes = (blocks / scale).astype(np.float32).astype(dtype).astype(np.float64)
    return np.moveaxis((codes * scale).reshape(v.shape), -1, axis)


WIDE = False


def mx_kscale(k):
    if not WIDE:
        return np.ones(k)
    levels = np.array([18, -18])
    if k % 512:
        return np.exp2(np.random.permutation(np.resize(levels, k // 32))).repeat(32)
    a = np.empty((k // 512, 16))
    for p in range(k // 512):
        a[p, :8] = np.random.permutation(np.resize(levels, 8))
        for g in range(8):
            far = levels[np.abs(levels - a[p, g]) >= 10]
            a[p, g + 8] = far[np.random.randint(len(far))]
    return np.exp2(a.ravel()).repeat(32)


def f64(x):
    return np.asarray(x).astype(np.float64)


def striped(idx):
    return np.tile(np.asarray(idx).reshape(-1, 16).T, (8, 1)).astype(np.uint16)


def unstriped(offs):
    return offs[:16].T.reshape(-1).astype(np.int64)


def setup_inputs():
    n = np.random.standard_normal
    uni = np.random.uniform
    idx = np.random.permutation(2048)[:512]
    seg = np.random.permutation(1024)[:512]
    f_e = mx_kscale(512)
    return {
        "aT": (0.2 + n((512, 2048))).astype(np.float32),
        "bT": (0.5 * n((512, 1024))).astype(np.float32),
        "W": (n((512, 512)) / np.sqrt(512) * f_e[:, None]).astype(np.float32),
        "dz": (n((512, 512)) / f_e[:, None]).astype(np.float32),
        "gam": np.tile(uni(0.75, 1.3, 512), (128, 1)).astype(np.float32),
        "offs": striped(idx),
        "soffs": striped(seg),
    }


def reference(aT, bT, W, dz, gam, offs, soffs):
    idx = unstriped(offs)
    seg = unstriped(soffs)
    a = f64(aT)[:, idx]
    b = f64(bT)[:, seg]
    x = a + b
    xr = x.T
    dn = mxq(f64(dz), 0, "e5m2").T @ mxq(f64(W), 0, "e4m3")
    h = f64(gam)[:1] * dn
    s1 = (xr).sum(-1, keepdims=True)
    c = xr - s1 / 512.0
    s2 = (np.square(c)).sum(-1, keepdims=True)
    rstd = 1.0 / np.sqrt(s2 / 512.0)
    n = c * rstd
    h1 = (h).sum(-1, keepdims=True)
    h2 = (h * n).sum(-1, keepdims=True)
    dx = rstd * (h - h1 / 512.0 - n * h2 / 512.0)
    dxt = dx.T
    out_0 = np.zeros((512, 2048))
    out_0[:, idx] = dxt
    out_1 = np.zeros((512, 1024))
    out_1[:, seg] = dxt
    return out_0, out_1

@@ -1,0 +1,296 @@
+from contextlib import ExitStack
+
+import concourse.mybir as mybir
+from concourse.masks import make_identity
+
+F32 = mybir.dt.float32
+BF16 = mybir.dt.bfloat16
+U32 = mybir.dt.uint32
+I32 = mybir.dt.int32
+U16 = mybir.dt.uint16
+U8 = mybir.dt.uint8
+E4M3 = mybir.dt.float8_e4m3fn_x4
+E5M2 = mybir.dt.float8_e5m2_x4
+ALU = mybir.AluOpType
+ACT = mybir.ActivationFunctionType
+
+P = 128
+D = 512
+SLOTS = 512
+TOKENS = 2048
+SEGMENTS = 1024
+NB = 4
+HALF = 256
+FLOPS = 2 * 512 * 512 * 512
+
+
+def tile_attend_gtwoemb_ln_kernel(tc, aT, bT, W, dz, gam, offs, soffs, out_0, out_1):
+    nc = tc.nc
+    with ExitStack() as ctx:
+        keep = ctx.enter_context(tc.tile_pool(name="keep", bufs=1))
+        spare = ctx.enter_context(tc.tile_pool(name="spare", bufs=4))
+        psum = ctx.enter_context(tc.psum_pool(name="psum", bufs=1))
+
+        def bank(n, shape):
+            return psum.tile(shape, F32, name="bank", tag="bank%d" % n)
+
+        def stat(name):
+            return keep.tile([P, NB], F32, name=name)
+
+        def rows(k):
+            return slice(k * P, (k + 1) * P)
+
+        def turn(out, in_, start, stop):
+            nc.tensor.matmul(out, lhsT=in_, rhs=ident[:], start=start, stop=stop, is_transpose=True)
+
+        tok_list = keep.tile([P, SLOTS // 16], U16, name="tok_list")
+        seg_list = keep.tile([P, SLOTS // 16], U16, name="seg_list")
+        dz_raw = keep.tile([P, 4, SLOTS], F32, name="dz_raw")
+        w_raw = keep.tile([P, 4, D], F32, name="w_raw")
+        a_tab = [keep.tile([P, TOKENS], F32, name="a_tab%d" % k) for k in range(NB)]
+        b_tab = [keep.tile([P, SEGMENTS], F32, name="b_tab%d" % k) for k in range(NB)]
+        nc.sync.dma_start(out=dz_raw[:], in_=dz.rearrange("(p t) i -> p t i", t=4))
+        nc.sync.dma_start(out=w_raw[:], in_=W.rearrange("(p t) d -> p t d", t=4))
+        gam_rows = keep.tile([P, P], F32, name="gam_rows")
+        nc.sync.dma_start(out=gam_rows[:], in_=gam[0 : P // NB, :].rearrange("r (k c) -> (r k) c", k=NB))
+        nc.sync.dma_start(tok_list[:], offs)
+        nc.sync.dma_start(seg_list[:], soffs)
+        for k in range(NB):
+            nc.sync.dma_start(out=b_tab[k][:], in_=bT[rows(k), :])
+            nc.sync.dma_start(out=a_tab[k][:], in_=aT[rows(k), :])
+
+        ident = keep.tile([P, P], F32, name="ident")
+        make_identity(nc, ident[:])
+
+        one = keep.tile([P, 1], F32, name="one")
+        warm = keep.tile([P, 1], F32, name="warm")
+        nc.gpsimd.memset(one[:], 1.0)
+        nc.scalar.activation(warm[:], one[:], ACT.Sqrt)
+
+        tok_win = [keep.tile([P, TOKENS], F32, name="tok_win%d" % n) for n in range(3)]
+        seg_win = [keep.tile([P, SEGMENTS], F32, name="seg_win%d" % n) for n in range(2)]
+
+        gam_ps = bank(7, [P, P])
+        turn(gam_ps[:], gam_rows[:], True, True)
+        gam_col = stat("gam_col")
+        nc.scalar.copy(gam_col[:], gam_ps[:, 0:NB])
+        gam_spread = bank(6, [P, D])
+        for k in range(NB):
+            turn(gam_spread[:, rows(k)], gam_col[:, k : k + 1].to_broadcast([P, P]), True, True)
+        gam_all = keep.tile([P, D], F32, name="gam_all")
+        nc.scalar.copy(gam_all[:], gam_spread[:])
+
+        def quantise(raw, name, fmt, copy):
+            woven = keep.tile([P, 512, 4], BF16, name=name + "_woven", align_bytes=64)
+            codes = keep.tile([P, 512], U32, name=name + "_codes", align_bytes=64)
+            scales = keep.tile([P, 512], U8, name=name + "_scales", align_bytes=64)
+            copy(
+                out=woven[:].rearrange("p (c i) t -> p c t i", i=4),
+                in_=raw[:].rearrange("p t (c i) -> p c t i", i=4),
+            )
+            nc.vector.quantize_mx(
+                out=codes[:].bitcast(fmt), scales=scales[:], in_=woven[:].rearrange("p c t -> p (c t)")
+            )
+            return codes, scales
+
+        dz_codes, dz_scales = quantise(dz_raw, "dz", E5M2, nc.scalar.copy)
+        w_codes, w_scales = quantise(w_raw, "w", E4M3, nc.vector.tensor_copy)
+
+        a_got = [keep.tile([P, SLOTS], F32, name="a_got%d" % k) for k in range(NB)]
+        b_got = [keep.tile([P, SLOTS], F32, name="b_got%d" % k) for k in range(NB)]
+        x_id = [keep.tile([P, D], F32, name="x_id%d" % j) for j in range(NB)]
+        s1 = [stat("s1_%d" % k) for k in range(NB)]
+        s2 = [stat("s2_%d" % k) for k in range(NB)]
+        all_hx = stat("all_hx")
+        neg_shift = stat("neg_shift")
+
+        def sum_x(k, j, src):
+            nc.scalar.activation(x_id[j][:, rows(k)], src, ACT.Copy, accum_out=s1[k][:, j : j + 1])
+
+        def sum_squares(k, j, src):
+            squares = spare.tile([P, P], F32, name="squares")
+            nc.scalar.activation(
+                squares[:], src, ACT.Square, bias=neg_shift[:, j : j + 1], accum_out=s2[k][:, j : j + 1]
+            )
+
+        def sum_hx(j):
+            products = spare.tile([P, D], F32, name="products")
+            nc.vector.scalar_tensor_tensor(
+                products[:],
+                x_id[j][:],
+                neg_shift[:, j : j + 1],
+                h_id[j][:],
+                ALU.add,
+                ALU.mult,
+                accum_out=all_hx[:, j : j + 1],
+            )
+
+        for k in range(NB - 1):
+            nc.vector.tensor_copy(b_got[k][:], b_tab[k][:].indirect(seg_list[:]))
+            nc.vector.tensor_copy(a_got[k][:], a_tab[k][:].indirect(tok_list[:]))
+            block = bank(4 + k % 2, [P, NB, P])
+            for n, got in enumerate((b_got[k], a_got[k])):
+                for j in range(NB):
+                    turn(block[:, j, :], got[:, rows(j)], n == 0 and j == 0, n == 1 and j == NB - 1)
+            for j in range(NB):
+                sum_x(k, j, block[:, j, :])
+            if k == 0:
+                nc.scalar.mul(neg_shift[:], s1[0][:], -1.0 / P)
+            for j in range(NB):
+                sum_squares(k, j, block[:, j, :])
+        nc.vector.tensor_copy(b_got[3][:], b_tab[3][:].indirect(seg_list[:]))
+        for jp in range(2):
+            nc.vector.tensor_copy(
+                a_got[3][:, jp * HALF : (jp + 1) * HALF], a_tab[3][:].indirect(tok_list[:, jp * 16 : (jp + 1) * 16])
+            )
+
+        h_id = [keep.tile([P, D], F32, name="h_id%d" % j) for j in range(NB)]
+        h1 = stat("h1")
+        for j in range(NB):
+            dn = bank(j, [P, D])
+            nc.tensor.matmul_mx(
+                out=dn[:],
+                lhsT=dz_codes[:, rows(j)].bitcast(E5M2),
+                lhsT_scale=dz_scales[:, rows(j)],
+                rhs=w_codes[:].bitcast(E4M3),
+                rhs_scale=w_scales[:],
+                start=True,
+                stop=True,
+            )
+            nc.vector.scalar_tensor_tensor(
+                h_id[j][:], dn[:], 1.0, gam_all[:], ALU.mult, ALU.mult, accum_out=h1[:, j : j + 1]
+            )
+        neg_h1n = stat("neg_h1n")
+        nc.gpsimd.tensor_scalar(neg_h1n[:], h1[:], -1.0 / D, 0.0, ALU.mult, ALU.add)
+
+        sums = {}
+        for jp in range(2):
+            for kp in range(2):
+                acc = bank(2 * jp + kp, [P, 2, 2, P])
+                sums[jp, kp] = acc
+                for kk in range(2):
+                    for jj in range(2):
+                        turn(acc[:, kk, jj, :], h_id[2 * jp + jj][:, rows(2 * kp + kk)], kk + jj == 0, False)
+
+        for win in (tok_win[0], seg_win[0], seg_win[1]):
+            nc.vector.memset(win[:].bitcast(I32), 0)
+        for win in (tok_win[1], tok_win[2]):
+            nc.gpsimd.memset(win[:].bitcast(I32), 0)
+
+        pair_s1 = stat("pair_s1")
+        pair_s2 = stat("pair_s2")
+        early_s1 = stat("early_s1")
+        early_neg_dev = stat("early_neg_dev")
+        early_s2 = stat("early_s2")
+        first_s1 = stat("first_s1")
+        nc.gpsimd.tensor_scalar(first_s1[:], s1[0][:], -3.0, 0.0, ALU.mult, ALU.add)
+        nc.gpsimd.tensor_tensor(pair_s1[:], first_s1[:], s1[1][:], ALU.add)
+        nc.gpsimd.tensor_tensor(pair_s2[:], s2[0][:], s2[1][:], ALU.add)
+        nc.gpsimd.tensor_tensor(early_s1[:], pair_s1[:], s1[2][:], ALU.add)
+        nc.gpsimd.tensor_scalar(early_neg_dev[:], early_s1[:], -1.0 / D, 0.0, ALU.mult, ALU.add)
+        nc.gpsimd.tensor_tensor(early_s2[:], pair_s2[:], s2[2][:], ALU.add)
+
+        dev_d = stat("dev_d")
+        neg_dev = stat("neg_dev")
+        all_s2 = stat("all_s2")
+        var_d = stat("var_d")
+        inv_var_d = stat("inv_var_d")
+        hc = stat("hc")
+        mean = stat("mean")
+        hc_mean = stat("hc_mean")
+        slope = stat("slope")
+        offset = stat("offset")
+        rstd = stat("rstd")
+        v_id = [keep.tile([P, D], F32, name="v_id%d" % j) for j in range(NB)]
+        rstd_rows = keep.tile([P, SLOTS], F32, name="rstd_rows")
+        w_first = [keep.tile([P, 2, HALF], F32, name="w_first%d" % jp) for jp in range(2)]
+        w_second = keep.tile([P, 2, SLOTS], F32, name="w_second")
+
+        def finish_stats(jp):
+            pair = slice(2 * jp, 2 * jp + 2)
+            tiles = (2 * jp, 2 * jp + 1)
+            last = bank((7, 5)[jp], [P, 2, P])
+            for n, got in enumerate((b_got[3], a_got[3])):
+                for j in tiles:
+                    turn(last[:, j % 2, :], got[:, rows(j)], n == 0 and j % 2 == 0, n == 1 and j % 2 == 1)
+            for j in tiles:
+                sum_x(3, j, last[:, j % 2, :])
+            for j in tiles:
+                sum_squares(3, j, last[:, j % 2, :])
+            for j in tiles:
+                sum_hx(j)
+            nc.vector.tensor_tensor(dev_d[:, pair], s1[3][:, pair], early_s1[:, pair], ALU.add)
+            nc.vector.scalar_tensor_tensor(
+                neg_dev[:, pair], s1[3][:, pair], -1.0 / D, early_neg_dev[:, pair], ALU.mult, ALU.add
+            )
+            nc.vector.tensor_tensor(all_s2[:, pair], s2[3][:, pair], early_s2[:, pair], ALU.add)
+            for j in tiles:
+                col = slice(j, j + 1)
+                nc.vector.scalar_tensor_tensor(
+                    var_d[:, col], dev_d[:, col], neg_dev[:, col], all_s2[:, col], ALU.mult, ALU.add
+                )
+            for j in tiles:
+                col = slice(j, j + 1)
+                nc.vector.scalar_tensor_tensor(
+                    hc[:, col], h1[:, col], neg_dev[:, col], all_hx[:, col], ALU.mult, ALU.add
+                )
+            nc.vector.scalar_tensor_tensor(
+                mean[:, pair], neg_dev[:, pair], -1.0, neg_shift[:, pair], ALU.mult, ALU.subtract
+            )
+            nc.vector.reciprocal(inv_var_d[:, pair], var_d[:, pair])
+            nc.vector.tensor_tensor(hc_mean[:, pair], hc[:, pair], mean[:, pair], ALU.mult)
+            nc.vector.scalar_tensor_tensor(slope[:, pair], hc[:, pair], -1.0, inv_var_d[:, pair], ALU.mult, ALU.mult)
+            for j in tiles:
+                col = slice(j, j + 1)
+                nc.vector.scalar_tensor_tensor(
+                    offset[:, col], hc_mean[:, col], inv_var_d[:, col], neg_h1n[:, col], ALU.mult, ALU.add
+                )
+            nc.scalar.activation(rstd[:, pair], inv_var_d[:, pair], ACT.Sqrt, scale=float(D))
+            spread = bank((6, 4)[jp], [P, 2, P])
+            for j in tiles:
+                turn(spread[:, j % 2, :], rstd[:, j : j + 1].to_broadcast([P, P]), True, True)
+            nc.scalar.copy(rstd_rows[:, jp * HALF : (jp + 1) * HALF], spread[:].rearrange("p a b -> p (a b)"))
+
+        def finish_sum(jp, kp, on_vector):
+            cols = slice(kp * HALF, (kp + 1) * HALF)
+            for j in (2 * jp, 2 * jp + 1):
+                col = slice(j, j + 1)
+                if on_vector:
+                    nc.vector.tensor_scalar(
+                        v_id[j][:, cols], x_id[j][:, cols], slope[:, col], offset[:, col], ALU.mult, ALU.add
+                    )
+                else:
+                    nc.scalar.activation(
+                        v_id[j][:, cols], x_id[j][:, cols], ACT.Identity, bias=offset[:, col], scale=slope[:, col]
+                    )
+            acc = sums[jp, kp]
+            for kk in range(2):
+                for jj in range(2):
+                    turn(acc[:, kk, jj, :], v_id[2 * jp + jj][:, rows(2 * kp + kk)], False, kk + jj == 2)
+            target = w_first[jp][:] if kp == 0 else w_second[:, :, jp * HALF : (jp + 1) * HALF]
+            nc.scalar.copy(target, acc[:].rearrange("p k a b -> p k (a b)"))
+
+        finish_stats(0)
+        finish_sum(0, 0, True)
+        probe2 = keep.tile([P, 1], F32, name="probe2")
+        nc.gpsimd.tensor_copy(probe2[:], w_first[0][:, 0, 0:1])
+        finish_stats(1)
+        finish_sum(1, 0, False)
+        finish_sum(0, 1, False)
+        finish_sum(1, 1, False)
+
+        for jp in range(2):
+            part = slice(jp * 16, (jp + 1) * 16)
+            factor = rstd_rows[:, jp * HALF : (jp + 1) * HALF]
+            for k in range(2):
+                nc.vector.tensor_tensor(tok_win[k][:].indirect(tok_list[:, part]), w_first[jp][:, k, :], factor, ALU.mult)
+                if jp == 1:
+                    nc.sync.dma_start(out=out_0[rows(k), :], in_=tok_win[k][:])
+                nc.vector.tensor_tensor(seg_win[k][:].indirect(seg_list[:, part]), w_first[jp][:, k, :], factor, ALU.mult)
+                if jp == 1:
+                    nc.sync.dma_start(out=out_1[rows(k), :], in_=seg_win[k][:])
+        for k in range(2, NB):
+            nc.vector.tensor_tensor(tok_win[k % 3][:].indirect(tok_list[:]), w_second[:, k - 2, :], rstd_rows[:], ALU.mult)
+            nc.sync.dma_start(out=out_0[rows(k), :], in_=tok_win[k % 3][:])
+            nc.vector.tensor_tensor(seg_win[k % 2][:].indirect(seg_list[:]), w_second[:, k - 2, :], rstd_rows[:], ALU.mult)
+            nc.sync.dma_start(out=out_1[rows(k), :], in_=seg_win[k % 2][:])

@@ -21,6 +21,7 @@ TOKENS = 2048
 SEGMENTS = 1024
 NB = 4
 HALF = 256
+VECTOR_COLS = 336
 FLOPS = 2 * 512 * 512 * 512
 
 
@@ -49,10 +50,10 @@ def tile_attend_gtwoemb_ln_kernel(tc, aT, bT, W, dz, gam, offs, soffs, out_0, ou
         w_raw = keep.tile([P, 4, D], F32, name="w_raw")
         a_tab = [keep.tile([P, TOKENS], F32, name="a_tab%d" % k) for k in range(NB)]
         b_tab = [keep.tile([P, SEGMENTS], F32, name="b_tab%d" % k) for k in range(NB)]
-        nc.sync.dma_start(out=dz_raw[:], in_=dz.rearrange("(p t) i -> p t i", t=4))
-        nc.sync.dma_start(out=w_raw[:], in_=W.rearrange("(p t) d -> p t d", t=4))
-        gam_rows = keep.tile([P, P], F32, name="gam_rows")
+        gam_rows = keep.tile([P, P], F32, name="gam_rows", tag="tok_win1")
         nc.sync.dma_start(out=gam_rows[:], in_=gam[0 : P // NB, :].rearrange("r (k c) -> (r k) c", k=NB))
+        nc.sync.dma_start(out=w_raw[:], in_=W.rearrange("(p t) d -> p t d", t=4))
+        nc.sync.dma_start(out=dz_raw[:], in_=dz.rearrange("(p t) i -> p t i", t=4))
         nc.sync.dma_start(tok_list[:], offs)
         nc.sync.dma_start(seg_list[:], soffs)
         for k in range(NB):
@@ -62,13 +63,11 @@ def tile_attend_gtwoemb_ln_kernel(tc, aT, bT, W, dz, gam, offs, soffs, out_0, ou
         ident = keep.tile([P, P], F32, name="ident")
         make_identity(nc, ident[:])
 
-        one = keep.tile([P, 1], F32, name="one")
-        warm = keep.tile([P, 1], F32, name="warm")
-        nc.gpsimd.memset(one[:], 1.0)
-        nc.scalar.activation(warm[:], one[:], ACT.Sqrt)
+        count = keep.tile([P, 1], F32, name="count")
+        root_d = keep.tile([P, 1], F32, name="root_d")
+        nc.vector.memset(count[:], float(D))
+        nc.scalar.activation(root_d[:], count[:], ACT.Sqrt)
 
-        tok_win = [keep.tile([P, TOKENS], F32, name="tok_win%d" % n) for n in range(3)]
-        seg_win = [keep.tile([P, SEGMENTS], F32, name="seg_win%d" % n) for n in range(2)]
 
         gam_ps = bank(7, [P, P])
         turn(gam_ps[:], gam_rows[:], True, True)
@@ -80,49 +79,69 @@ def tile_attend_gtwoemb_ln_kernel(tc, aT, bT, W, dz, gam, offs, soffs, out_0, ou
         gam_all = keep.tile([P, D], F32, name="gam_all")
         nc.scalar.copy(gam_all[:], gam_spread[:])
 
-        def quantise(raw, name, fmt, copy):
+        def quantise(raw, name, fmt, shares):
             woven = keep.tile([P, 512, 4], BF16, name=name + "_woven", align_bytes=64)
             codes = keep.tile([P, 512], U32, name=name + "_codes", align_bytes=64)
             scales = keep.tile([P, 512], U8, name=name + "_scales", align_bytes=64)
-            copy(
-                out=woven[:].rearrange("p (c i) t -> p c t i", i=4),
-                in_=raw[:].rearrange("p t (c i) -> p c t i", i=4),
-            )
+            for copy, cols in shares:
+                copy(
+                    out=woven[:, cols, :].rearrange("p (c i) t -> p c t i", i=4),
+                    in_=raw[:, :, cols].rearrange("p t (c i) -> p c t i", i=4),
+                )
             nc.vector.quantize_mx(
                 out=codes[:].bitcast(fmt), scales=scales[:], in_=woven[:].rearrange("p c t -> p (c t)")
             )
             return codes, scales
 
-        dz_codes, dz_scales = quantise(dz_raw, "dz", E5M2, nc.scalar.copy)
-        w_codes, w_scales = quantise(w_raw, "w", E4M3, nc.vector.tensor_copy)
+        w_codes, w_scales = quantise(w_raw, "w", E4M3, [(nc.vector.tensor_copy, slice(0, D))])
+        dz_codes, dz_scales = quantise(
+            dz_raw, "dz", E5M2, [(nc.vector.tensor_copy, slice(0, VECTOR_COLS)), (nc.scalar.copy, slice(VECTOR_COLS, SLOTS))]
+        )
 
+        h_id = [keep.tile([P, D], F32, name="h_id%d" % j) for j in range(NB)]
+        h1 = stat("h1")
+        dn = [bank(j, [P, D]) for j in range(NB)]
+        for j in range(NB):
+            nc.tensor.matmul_mx(
+                out=dn[j][:],
+                lhsT=dz_codes[:, rows(j)].bitcast(E5M2),
+                lhsT_scale=dz_scales[:, rows(j)],
+                rhs=w_codes[:].bitcast(E4M3),
+                rhs_scale=w_scales[:],
+                start=True,
+                stop=True,
+            )
         a_got = [keep.tile([P, SLOTS], F32, name="a_got%d" % k) for k in range(NB)]
         b_got = [keep.tile([P, SLOTS], F32, name="b_got%d" % k) for k in range(NB)]
         x_id = [keep.tile([P, D], F32, name="x_id%d" % j) for j in range(NB)]
         s1 = [stat("s1_%d" % k) for k in range(NB)]
-        s2 = [stat("s2_%d" % k) for k in range(NB)]
+        s2 = [stat("s2_%d" % k) for k in range(3)]
         all_hx = stat("all_hx")
         neg_shift = stat("neg_shift")
+        shift = stat("shift")
 
         def sum_x(k, j, src):
             nc.scalar.activation(x_id[j][:, rows(k)], src, ACT.Copy, accum_out=s1[k][:, j : j + 1])
 
-        def sum_squares(k, j, src):
-            squares = spare.tile([P, P], F32, name="squares")
+        def sum_squares(k, j, width, src):
+            squares = spare.tile([P, HALF], F32, name="squares")
             nc.scalar.activation(
-                squares[:], src, ACT.Square, bias=neg_shift[:, j : j + 1], accum_out=s2[k][:, j : j + 1]
+                squares[:, 0:width], src, ACT.Square, bias=neg_shift[:, j : j + 1], accum_out=s2[k][:, j : j + 1]
             )
 
-        def sum_hx(j):
-            products = spare.tile([P, D], F32, name="products")
+        def sum_hx(j, cols, total):
+            if j < 2:
+                products = spare.tile([P, D], F32, name="products")
+            else:
+                products = keep.tile([P, D], F32, name="products", tag="x_id%d" % (j - 2))
             nc.vector.scalar_tensor_tensor(
-                products[:],
-                x_id[j][:],
+                products[:, cols],
+                x_id[j][:, cols],
                 neg_shift[:, j : j + 1],
-                h_id[j][:],
+                h_id[j][:, cols],
                 ALU.add,
                 ALU.mult,
-                accum_out=all_hx[:, j : j + 1],
+                accum_out=total[:, j : j + 1],
             )
 
         for k in range(NB - 1):
@@ -136,29 +155,19 @@ def tile_attend_gtwoemb_ln_kernel(tc, aT, bT, W, dz, gam, offs, soffs, out_0, ou
                 sum_x(k, j, block[:, j, :])
             if k == 0:
                 nc.scalar.mul(neg_shift[:], s1[0][:], -1.0 / P)
-            for j in range(NB):
-                sum_squares(k, j, block[:, j, :])
+                nc.scalar.mul(shift[:], s1[0][:], 1.0 / P)
+            if k < 2:
+                for j in range(NB):
+                    sum_squares(k, j, P, block[:, j, :])
         nc.vector.tensor_copy(b_got[3][:], b_tab[3][:].indirect(seg_list[:]))
         for jp in range(2):
             nc.vector.tensor_copy(
                 a_got[3][:, jp * HALF : (jp + 1) * HALF], a_tab[3][:].indirect(tok_list[:, jp * 16 : (jp + 1) * 16])
             )
 
-        h_id = [keep.tile([P, D], F32, name="h_id%d" % j) for j in range(NB)]
-        h1 = stat("h1")
         for j in range(NB):
-            dn = bank(j, [P, D])
-            nc.tensor.matmul_mx(
-                out=dn[:],
-                lhsT=dz_codes[:, rows(j)].bitcast(E5M2),
-                lhsT_scale=dz_scales[:, rows(j)],
-                rhs=w_codes[:].bitcast(E4M3),
-                rhs_scale=w_scales[:],
-                start=True,
-                stop=True,
-            )
             nc.vector.scalar_tensor_tensor(
-                h_id[j][:], dn[:], 1.0, gam_all[:], ALU.mult, ALU.mult, accum_out=h1[:, j : j + 1]
+                h_id[j][:], dn[j][:], 1.0, gam_all[:], ALU.mult, ALU.mult, accum_out=h1[:, j : j + 1]
             )
         neg_h1n = stat("neg_h1n")
         nc.gpsimd.tensor_scalar(neg_h1n[:], h1[:], -1.0 / D, 0.0, ALU.mult, ALU.add)
@@ -172,23 +181,23 @@ def tile_attend_gtwoemb_ln_kernel(tc, aT, bT, W, dz, gam, offs, soffs, out_0, ou
                     for jj in range(2):
                         turn(acc[:, kk, jj, :], h_id[2 * jp + jj][:, rows(2 * kp + kk)], kk + jj == 0, False)
 
+        tok_win = [keep.tile([P, TOKENS], F32, name="tok_win%d" % n) for n in range(2)]
+        seg_win = [keep.tile([P, SEGMENTS], F32, name="seg_win%d" % n) for n in range(2)]
         for win in (tok_win[0], seg_win[0], seg_win[1]):
             nc.vector.memset(win[:].bitcast(I32), 0)
-        for win in (tok_win[1], tok_win[2]):
+        for win in (tok_win[1],):
             nc.gpsimd.memset(win[:].bitcast(I32), 0)
 
         pair_s1 = stat("pair_s1")
-        pair_s2 = stat("pair_s2")
         early_s1 = stat("early_s1")
         early_neg_dev = stat("early_neg_dev")
         early_s2 = stat("early_s2")
         first_s1 = stat("first_s1")
         nc.gpsimd.tensor_scalar(first_s1[:], s1[0][:], -3.0, 0.0, ALU.mult, ALU.add)
         nc.gpsimd.tensor_tensor(pair_s1[:], first_s1[:], s1[1][:], ALU.add)
-        nc.gpsimd.tensor_tensor(pair_s2[:], s2[0][:], s2[1][:], ALU.add)
+        nc.gpsimd.tensor_tensor(early_s2[:], s2[0][:], s2[1][:], ALU.add)
         nc.gpsimd.tensor_tensor(early_s1[:], pair_s1[:], s1[2][:], ALU.add)
         nc.gpsimd.tensor_scalar(early_neg_dev[:], early_s1[:], -1.0 / D, 0.0, ALU.mult, ALU.add)
-        nc.gpsimd.tensor_tensor(early_s2[:], pair_s2[:], s2[2][:], ALU.add)
 
         dev_d = stat("dev_d")
         neg_dev = stat("neg_dev")
@@ -201,10 +210,14 @@ def tile_attend_gtwoemb_ln_kernel(tc, aT, bT, W, dz, gam, offs, soffs, out_0, ou
         slope = stat("slope")
         offset = stat("offset")
         rstd = stat("rstd")
-        v_id = [keep.tile([P, D], F32, name="v_id%d" % j) for j in range(NB)]
         rstd_rows = keep.tile([P, SLOTS], F32, name="rstd_rows")
         w_first = [keep.tile([P, 2, HALF], F32, name="w_first%d" % jp) for jp in range(2)]
         w_second = keep.tile([P, 2, SLOTS], F32, name="w_second")
+
+        neg_inv = stat("neg_inv")
+
+        def affine(out, in_, scale, bias):
+            nc.scalar.activation(out, in_, ACT.Identity, bias=bias, scale=scale)
 
         def finish_stats(jp):
             pair = slice(2 * jp, 2 * jp + 2)
@@ -216,67 +229,103 @@ def tile_attend_gtwoemb_ln_kernel(tc, aT, bT, W, dz, gam, offs, soffs, out_0, ou
             for j in tiles:
                 sum_x(3, j, last[:, j % 2, :])
             for j in tiles:
-                sum_squares(3, j, last[:, j % 2, :])
+                sum_squares(2, j, HALF, x_id[j][:, HALF:D])
             for j in tiles:
-                sum_hx(j)
-            nc.vector.tensor_tensor(dev_d[:, pair], s1[3][:, pair], early_s1[:, pair], ALU.add)
-            nc.vector.scalar_tensor_tensor(
-                neg_dev[:, pair], s1[3][:, pair], -1.0 / D, early_neg_dev[:, pair], ALU.mult, ALU.add
+                sum_hx(j, slice(0, D), all_hx)
+            if jp == 0:
+                nc.vector.tensor_tensor(dev_d[:, pair], s1[3][:, pair], early_s1[:, pair], ALU.add)
+                nc.vector.scalar_tensor_tensor(
+                    neg_dev[:, pair], s1[3][:, pair], -1.0 / D, early_neg_dev[:, pair], ALU.mult, ALU.add
+                )
+                nc.vector.tensor_tensor(all_s2[:, pair], s2[2][:, pair], early_s2[:, pair], ALU.add)
+                for j in tiles:
+                    col = slice(j, j + 1)
+                    nc.vector.scalar_tensor_tensor(
+                        var_d[:, col], dev_d[:, col], neg_dev[:, col], all_s2[:, col], ALU.mult, ALU.add
+                    )
+                for j in tiles:
+                    col = slice(j, j + 1)
+                    nc.vector.scalar_tensor_tensor(
+                        hc[:, col], h1[:, col], neg_dev[:, col], all_hx[:, col], ALU.mult, ALU.add
+                    )
+                nc.vector.scalar_tensor_tensor(
+                    mean[:, pair], neg_dev[:, pair], -1.0, neg_shift[:, pair], ALU.mult, ALU.subtract
+                )
+                nc.vector.reciprocal(inv_var_d[:, pair], var_d[:, pair])
+                nc.scalar.activation(rstd[:, pair], inv_var_d[:, pair], ACT.Sqrt)
+                nc.vector.tensor_tensor(hc_mean[:, pair], hc[:, pair], mean[:, pair], ALU.mult)
+                nc.vector.scalar_tensor_tensor(slope[:, pair], hc[:, pair], -1.0, inv_var_d[:, pair], ALU.mult, ALU.mult)
+                for j in tiles:
+                    col = slice(j, j + 1)
+                    nc.vector.scalar_tensor_tensor(
+                        offset[:, col], hc_mean[:, col], inv_var_d[:, col], neg_h1n[:, col], ALU.mult, ALU.add
+                    )
+            else:
+                for step in range(3):
+                    for j in tiles:
+                        col = slice(j, j + 1)
+                        if step == 0:
+                            affine(dev_d[:, col], s1[3][:, col], 1.0, early_s1[:, col])
+                            affine(neg_dev[:, col], s1[3][:, col], -1.0 / D, early_neg_dev[:, col])
+                            affine(all_s2[:, col], s2[2][:, col], 1.0, early_s2[:, col])
+                        if step == 1:
+                            affine(var_d[:, col], dev_d[:, col], neg_dev[:, col], all_s2[:, col])
+                            affine(mean[:, col], neg_dev[:, col], -1.0, shift[:, col])
+                        if step == 2:
+                            affine(hc[:, col], h1[:, col], neg_dev[:, col], all_hx[:, col])
+                nc.vector.reciprocal(inv_var_d[:, pair], var_d[:, pair])
+                nc.scalar.activation(rstd[:, pair], inv_var_d[:, pair], ACT.Sqrt)
+                nc.scalar.mul(neg_inv[:, pair], inv_var_d[:, pair], -1.0)
+                for j in tiles:
+                    col = slice(j, j + 1)
+                    nc.scalar.activation(hc_mean[:, col], hc[:, col], ACT.Copy, scale=mean[:, col])
+                for j in tiles:
+                    col = slice(j, j + 1)
+                    nc.scalar.activation(slope[:, col], hc[:, col], ACT.Copy, scale=neg_inv[:, col])
+                for j in tiles:
+                    col = slice(j, j + 1)
+                    affine(offset[:, col], hc_mean[:, col], inv_var_d[:, col], neg_h1n[:, col])
+
+        def spread_rstd(jp):
+            spread = bank((6, 0)[jp], [P, 2, P])
+            for jj in range(2):
+                j = 2 * jp + jj
+                turn(spread[:, jj, :], rstd[:, j : j + 1].to_broadcast([P, P]), True, True)
+            nc.scalar.activation(
+                rstd_rows[:, jp * HALF : (jp + 1) * HALF],
+                spread[:].rearrange("p a b -> p (a b)"),
+                ACT.Copy,
+                scale=root_d[:],
             )
-            nc.vector.tensor_tensor(all_s2[:, pair], s2[3][:, pair], early_s2[:, pair], ALU.add)
-            for j in tiles:
-                col = slice(j, j + 1)
-                nc.vector.scalar_tensor_tensor(
-                    var_d[:, col], dev_d[:, col], neg_dev[:, col], all_s2[:, col], ALU.mult, ALU.add
-                )
-            for j in tiles:
-                col = slice(j, j + 1)
-                nc.vector.scalar_tensor_tensor(
-                    hc[:, col], h1[:, col], neg_dev[:, col], all_hx[:, col], ALU.mult, ALU.add
-                )
-            nc.vector.scalar_tensor_tensor(
-                mean[:, pair], neg_dev[:, pair], -1.0, neg_shift[:, pair], ALU.mult, ALU.subtract
-            )
-            nc.vector.reciprocal(inv_var_d[:, pair], var_d[:, pair])
-            nc.vector.tensor_tensor(hc_mean[:, pair], hc[:, pair], mean[:, pair], ALU.mult)
-            nc.vector.scalar_tensor_tensor(slope[:, pair], hc[:, pair], -1.0, inv_var_d[:, pair], ALU.mult, ALU.mult)
-            for j in tiles:
-                col = slice(j, j + 1)
-                nc.vector.scalar_tensor_tensor(
-                    offset[:, col], hc_mean[:, col], inv_var_d[:, col], neg_h1n[:, col], ALU.mult, ALU.add
-                )
-            nc.scalar.activation(rstd[:, pair], inv_var_d[:, pair], ACT.Sqrt, scale=float(D))
-            spread = bank((6, 4)[jp], [P, 2, P])
-            for j in tiles:
-                turn(spread[:, j % 2, :], rstd[:, j : j + 1].to_broadcast([P, P]), True, True)
-            nc.scalar.copy(rstd_rows[:, jp * HALF : (jp + 1) * HALF], spread[:].rearrange("p a b -> p (a b)"))
 
         def finish_sum(jp, kp, on_vector):
             cols = slice(kp * HALF, (kp + 1) * HALF)
+            v_id = {}
             for j in (2 * jp, 2 * jp + 1):
+                v_id[j] = keep.tile([P, HALF], F32, name="v_id", tag="v_id%d_%d" % (j % 2, kp))
                 col = slice(j, j + 1)
                 if on_vector:
                     nc.vector.tensor_scalar(
-                        v_id[j][:, cols], x_id[j][:, cols], slope[:, col], offset[:, col], ALU.mult, ALU.add
+                        v_id[j][:], x_id[j][:, cols], slope[:, col], offset[:, col], ALU.mult, ALU.add
                     )
                 else:
                     nc.scalar.activation(
-                        v_id[j][:, cols], x_id[j][:, cols], ACT.Identity, bias=offset[:, col], scale=slope[:, col]
+                        v_id[j][:], x_id[j][:, cols], ACT.Identity, bias=offset[:, col], scale=slope[:, col]
                     )
             acc = sums[jp, kp]
             for kk in range(2):
                 for jj in range(2):
-                    turn(acc[:, kk, jj, :], v_id[2 * jp + jj][:, rows(2 * kp + kk)], False, kk + jj == 2)
+                    turn(acc[:, kk, jj, :], v_id[2 * jp + jj][:, rows(kk)], False, kk + jj == 2)
             target = w_first[jp][:] if kp == 0 else w_second[:, :, jp * HALF : (jp + 1) * HALF]
             nc.scalar.copy(target, acc[:].rearrange("p k a b -> p k (a b)"))
 
         finish_stats(0)
+        spread_rstd(0)
         finish_sum(0, 0, True)
-        probe2 = keep.tile([P, 1], F32, name="probe2")
-        nc.gpsimd.tensor_copy(probe2[:], w_first[0][:, 0, 0:1])
-        finish_stats(1)
-        finish_sum(1, 0, False)
         finish_sum(0, 1, False)
+        finish_stats(1)
+        spread_rstd(1)
+        finish_sum(1, 0, False)
         finish_sum(1, 1, False)
 
         for jp in range(2):
@@ -290,7 +339,7 @@ def tile_attend_gtwoemb_ln_kernel(tc, aT, bT, W, dz, gam, offs, soffs, out_0, ou
                 if jp == 1:
                     nc.sync.dma_start(out=out_1[rows(k), :], in_=seg_win[k][:])
         for k in range(2, NB):
-            nc.vector.tensor_tensor(tok_win[k % 3][:].indirect(tok_list[:]), w_second[:, k - 2, :], rstd_rows[:], ALU.mult)
-            nc.sync.dma_start(out=out_0[rows(k), :], in_=tok_win[k % 3][:])
+            nc.vector.tensor_tensor(tok_win[k % 2][:].indirect(tok_list[:]), w_second[:, k - 2, :], rstd_rows[:], ALU.mult)
+            nc.sync.dma_start(out=out_0[rows(k), :], in_=tok_win[k % 2][:])
             nc.vector.tensor_tensor(seg_win[k % 2][:].indirect(seg_list[:]), w_second[:, k - 2, :], rstd_rows[:], ALU.mult)
             nc.sync.dma_start(out=out_1[rows(k), :], in_=seg_win[k % 2][:])

@@ -50,7 +50,7 @@ def tile_attend_gtwoemb_ln_kernel(tc, aT, bT, W, dz, gam, offs, soffs, out_0, ou
         w_raw = keep.tile([P, 4, D], F32, name="w_raw")
         a_tab = [keep.tile([P, TOKENS], F32, name="a_tab%d" % k) for k in range(NB)]
         b_tab = [keep.tile([P, SEGMENTS], F32, name="b_tab%d" % k) for k in range(NB)]
-        gam_rows = keep.tile([P, P], F32, name="gam_rows", tag="tok_win1")
+        gam_rows = keep.tile([P, P], F32, name="gam_rows")
         nc.sync.dma_start(out=gam_rows[:], in_=gam[0 : P // NB, :].rearrange("r (k c) -> (r k) c", k=NB))
         nc.sync.dma_start(out=w_raw[:], in_=W.rearrange("(p t) d -> p t d", t=4))
         nc.sync.dma_start(out=dz_raw[:], in_=dz.rearrange("(p t) i -> p t i", t=4))
@@ -129,11 +129,9 @@ def tile_attend_gtwoemb_ln_kernel(tc, aT, bT, W, dz, gam, offs, soffs, out_0, ou
                 squares[:, 0:width], src, ACT.Square, bias=neg_shift[:, j : j + 1], accum_out=s2[k][:, j : j + 1]
             )
 
-        def sum_hx(j, cols, total):
-            if j < 2:
+        def sum_hx(j, cols, total, products=None):
+            if products is None:
                 products = spare.tile([P, D], F32, name="products")
-            else:
-                products = keep.tile([P, D], F32, name="products", tag="x_id%d" % (j - 2))
             nc.vector.scalar_tensor_tensor(
                 products[:, cols],
                 x_id[j][:, cols],
@@ -172,20 +170,24 @@ def tile_attend_gtwoemb_ln_kernel(tc, aT, bT, W, dz, gam, offs, soffs, out_0, ou
         neg_h1n = stat("neg_h1n")
         nc.gpsimd.tensor_scalar(neg_h1n[:], h1[:], -1.0 / D, 0.0, ALU.mult, ALU.add)
 
+        groups = [(0, (0,), 0), (0, (1,), 6), (0, (2, 3), 1), (1, (0, 1), 2), (1, (2, 3), 3)]
         sums = {}
-        for jp in range(2):
-            for kp in range(2):
-                acc = bank(2 * jp + kp, [P, 2, 2, P])
-                sums[jp, kp] = acc
-                for kk in range(2):
-                    for jj in range(2):
-                        turn(acc[:, kk, jj, :], h_id[2 * jp + jj][:, rows(2 * kp + kk)], kk + jj == 0, False)
+        for jp, blocks, n in groups:
+            acc = bank(n, [P, len(blocks), 2, P])
+            sums[jp, blocks] = acc
+            for kk, k in enumerate(blocks):
+                for jj in range(2):
+                    turn(acc[:, kk, jj, :], h_id[2 * jp + jj][:, rows(k)], kk + jj == 0, False)
 
-        tok_win = [keep.tile([P, TOKENS], F32, name="tok_win%d" % n) for n in range(2)]
+        tok_win = [
+            keep.tile([P, TOKENS], F32, name="tok_win0"),
+            keep.tile([P, TOKENS], F32, name="tok_win1", tag="dz_woven", align_bytes=64),
+            keep.tile([P, TOKENS], F32, name="tok_win2", tag="dz_codes", align_bytes=64),
+        ]
         seg_win = [keep.tile([P, SEGMENTS], F32, name="seg_win%d" % n) for n in range(2)]
         for win in (tok_win[0], seg_win[0], seg_win[1]):
             nc.vector.memset(win[:].bitcast(I32), 0)
-        for win in (tok_win[1],):
+        for win in tok_win[1:]:
             nc.gpsimd.memset(win[:].bitcast(I32), 0)
 
         pair_s1 = stat("pair_s1")
@@ -206,7 +208,7 @@ def tile_attend_gtwoemb_ln_kernel(tc, aT, bT, W, dz, gam, offs, soffs, out_0, ou
         inv_var_d = stat("inv_var_d")
         hc = stat("hc")
         mean = stat("mean")
-        hc_mean = stat("hc_mean")
+        hc_mean = [keep.tile([P, 2], F32, name="hc_mean%d" % jp) for jp in range(2)]
         slope = stat("slope")
         offset = stat("offset")
         rstd = stat("rstd")
@@ -230,8 +232,10 @@ def tile_attend_gtwoemb_ln_kernel(tc, aT, bT, W, dz, gam, offs, soffs, out_0, ou
                 sum_x(3, j, last[:, j % 2, :])
             for j in tiles:
                 sum_squares(2, j, HALF, x_id[j][:, HALF:D])
+            if jp == 1:
+                held = keep.tile([P, 2, D], F32, name="held", tag="hc_mean0")
             for j in tiles:
-                sum_hx(j, slice(0, D), all_hx)
+                sum_hx(j, slice(0, D), all_hx, held[:, j % 2, :] if jp == 1 else None)
             if jp == 0:
                 nc.vector.tensor_tensor(dev_d[:, pair], s1[3][:, pair], early_s1[:, pair], ALU.add)
                 nc.vector.scalar_tensor_tensor(
@@ -253,41 +257,43 @@ def tile_attend_gtwoemb_ln_kernel(tc, aT, bT, W, dz, gam, offs, soffs, out_0, ou
                 )
                 nc.vector.reciprocal(inv_var_d[:, pair], var_d[:, pair])
                 nc.scalar.activation(rstd[:, pair], inv_var_d[:, pair], ACT.Sqrt)
-                nc.vector.tensor_tensor(hc_mean[:, pair], hc[:, pair], mean[:, pair], ALU.mult)
+                nc.vector.tensor_tensor(hc_mean[jp][:], hc[:, pair], mean[:, pair], ALU.mult)
                 nc.vector.scalar_tensor_tensor(slope[:, pair], hc[:, pair], -1.0, inv_var_d[:, pair], ALU.mult, ALU.mult)
                 for j in tiles:
                     col = slice(j, j + 1)
                     nc.vector.scalar_tensor_tensor(
-                        offset[:, col], hc_mean[:, col], inv_var_d[:, col], neg_h1n[:, col], ALU.mult, ALU.add
+                        offset[:, col], hc_mean[jp][:, j % 2 : j % 2 + 1], inv_var_d[:, col], neg_h1n[:, col], ALU.mult, ALU.add
                     )
             else:
-                for step in range(3):
-                    for j in tiles:
-                        col = slice(j, j + 1)
-                        if step == 0:
-                            affine(dev_d[:, col], s1[3][:, col], 1.0, early_s1[:, col])
-                            affine(neg_dev[:, col], s1[3][:, col], -1.0 / D, early_neg_dev[:, col])
-                            affine(all_s2[:, col], s2[2][:, col], 1.0, early_s2[:, col])
-                        if step == 1:
-                            affine(var_d[:, col], dev_d[:, col], neg_dev[:, col], all_s2[:, col])
-                            affine(mean[:, col], neg_dev[:, col], -1.0, shift[:, col])
-                        if step == 2:
-                            affine(hc[:, col], h1[:, col], neg_dev[:, col], all_hx[:, col])
+                nc.vector.tensor_tensor(dev_d[:, pair], s1[3][:, pair], early_s1[:, pair], ALU.add)
+                nc.vector.scalar_tensor_tensor(
+                    neg_dev[:, pair], s1[3][:, pair], -1.0 / D, early_neg_dev[:, pair], ALU.mult, ALU.add
+                )
+                nc.vector.tensor_tensor(all_s2[:, pair], s2[2][:, pair], early_s2[:, pair], ALU.add)
+                for j in tiles:
+                    col = slice(j, j + 1)
+                    nc.vector.scalar_tensor_tensor(
+                        var_d[:, col], dev_d[:, col], neg_dev[:, col], all_s2[:, col], ALU.mult, ALU.add
+                    )
                 nc.vector.reciprocal(inv_var_d[:, pair], var_d[:, pair])
                 nc.scalar.activation(rstd[:, pair], inv_var_d[:, pair], ACT.Sqrt)
                 nc.scalar.mul(neg_inv[:, pair], inv_var_d[:, pair], -1.0)
                 for j in tiles:
                     col = slice(j, j + 1)
-                    nc.scalar.activation(hc_mean[:, col], hc[:, col], ACT.Copy, scale=mean[:, col])
+                    affine(mean[:, col], neg_dev[:, col], -1.0, shift[:, col])
+                    affine(hc[:, col], h1[:, col], neg_dev[:, col], all_hx[:, col])
+                for j in tiles:
+                    col = slice(j, j + 1)
+                    nc.scalar.activation(hc_mean[jp][:, j % 2 : j % 2 + 1], hc[:, col], ACT.Copy, scale=mean[:, col])
                 for j in tiles:
                     col = slice(j, j + 1)
                     nc.scalar.activation(slope[:, col], hc[:, col], ACT.Copy, scale=neg_inv[:, col])
                 for j in tiles:
                     col = slice(j, j + 1)
-                    affine(offset[:, col], hc_mean[:, col], inv_var_d[:, col], neg_h1n[:, col])
+                    affine(offset[:, col], hc_mean[jp][:, j % 2 : j % 2 + 1], inv_var_d[:, col], neg_h1n[:, col])
 
         def spread_rstd(jp):
-            spread = bank((6, 0)[jp], [P, 2, P])
+            spread = bank((4, 0)[jp], [P, 2, P])
             for jj in range(2):
                 j = 2 * jp + jj
                 turn(spread[:, jj, :], rstd[:, j : j + 1].to_broadcast([P, P]), True, True)
@@ -298,35 +304,36 @@ def tile_attend_gtwoemb_ln_kernel(tc, aT, bT, W, dz, gam, offs, soffs, out_0, ou
                 scale=root_d[:],
             )
 
-        def finish_sum(jp, kp, on_vector):
-            cols = slice(kp * HALF, (kp + 1) * HALF)
+        def finish_sum(jp, blocks, on_vector):
+            cols = slice(blocks[0] * P, (blocks[-1] + 1) * P)
             v_id = {}
             for j in (2 * jp, 2 * jp + 1):
-                v_id[j] = keep.tile([P, HALF], F32, name="v_id", tag="v_id%d_%d" % (j % 2, kp))
+                v_id[j] = keep.tile([P, len(blocks), P], F32, name="v_id", tag="v_id%d_%d" % (j % 2, blocks[0]))
                 col = slice(j, j + 1)
+                flat = v_id[j][:].rearrange("p k c -> p (k c)")
                 if on_vector:
-                    nc.vector.tensor_scalar(
-                        v_id[j][:], x_id[j][:, cols], slope[:, col], offset[:, col], ALU.mult, ALU.add
-                    )
+                    nc.vector.tensor_scalar(flat, x_id[j][:, cols], slope[:, col], offset[:, col], ALU.mult, ALU.add)
                 else:
-                    nc.scalar.activation(
-                        v_id[j][:], x_id[j][:, cols], ACT.Identity, bias=offset[:, col], scale=slope[:, col]
-                    )
-            acc = sums[jp, kp]
-            for kk in range(2):
+                    affine(flat, x_id[j][:, cols], slope[:, col], offset[:, col])
+            acc = sums[jp, blocks]
+            for kk in range(len(blocks)):
                 for jj in range(2):
-                    turn(acc[:, kk, jj, :], v_id[2 * jp + jj][:, rows(kk)], False, kk + jj == 2)
-            target = w_first[jp][:] if kp == 0 else w_second[:, :, jp * HALF : (jp + 1) * HALF]
+                    turn(acc[:, kk, jj, :], v_id[2 * jp + jj][:, kk, :], False, kk == len(blocks) - 1 and jj == 1)
+            if blocks[0] >= 2:
+                target = w_second[:, :, jp * HALF : (jp + 1) * HALF]
+            else:
+                target = w_first[jp][:, blocks[0] : blocks[-1] + 1, :]
             nc.scalar.copy(target, acc[:].rearrange("p k a b -> p k (a b)"))
 
         finish_stats(0)
         spread_rstd(0)
-        finish_sum(0, 0, True)
-        finish_sum(0, 1, False)
+        finish_sum(0, (0,), True)
+        finish_sum(0, (1,), False)
+        finish_sum(0, (2, 3), False)
         finish_stats(1)
         spread_rstd(1)
-        finish_sum(1, 0, False)
-        finish_sum(1, 1, False)
+        finish_sum(1, (0, 1), False)
+        finish_sum(1, (2, 3), False)
 
         for jp in range(2):
             part = slice(jp * 16, (jp + 1) * 16)
@@ -339,7 +346,7 @@ def tile_attend_gtwoemb_ln_kernel(tc, aT, bT, W, dz, gam, offs, soffs, out_0, ou
                 if jp == 1:
                     nc.sync.dma_start(out=out_1[rows(k), :], in_=seg_win[k][:])
         for k in range(2, NB):
-            nc.vector.tensor_tensor(tok_win[k % 2][:].indirect(tok_list[:]), w_second[:, k - 2, :], rstd_rows[:], ALU.mult)
-            nc.sync.dma_start(out=out_0[rows(k), :], in_=tok_win[k % 2][:])
+            nc.vector.tensor_tensor(tok_win[k % 3][:].indirect(tok_list[:]), w_second[:, k - 2, :], rstd_rows[:], ALU.mult)
+            nc.sync.dma_start(out=out_0[rows(k), :], in_=tok_win[k % 3][:])
             nc.vector.tensor_tensor(seg_win[k % 2][:].indirect(seg_list[:]), w_second[:, k - 2, :], rstd_rows[:], ALU.mult)
             nc.sync.dma_start(out=out_1[rows(k), :], in_=seg_win[k % 2][:])

@@ -65,7 +65,7 @@ def tile_attend_gtwoemb_ln_kernel(tc, aT, bT, W, dz, gam, offs, soffs, out_0, ou
 
         count = keep.tile([P, 1], F32, name="count")
         root_d = keep.tile([P, 1], F32, name="root_d")
-        nc.vector.memset(count[:], float(D))
+        nc.vector.memset(count[:], float(D * D))
         nc.scalar.activation(root_d[:], count[:], ACT.Sqrt)
 
 
@@ -170,7 +170,7 @@ def tile_attend_gtwoemb_ln_kernel(tc, aT, bT, W, dz, gam, offs, soffs, out_0, ou
         neg_h1n = stat("neg_h1n")
         nc.gpsimd.tensor_scalar(neg_h1n[:], h1[:], -1.0 / D, 0.0, ALU.mult, ALU.add)
 
-        groups = [(0, (0,), 0), (0, (1,), 6), (0, (2, 3), 1), (1, (0, 1), 2), (1, (2, 3), 3)]
+        groups = [(0, (0,), 0), (0, (1,), 1), (1, (0, 1), 2)]
         sums = {}
         for jp, blocks, n in groups:
             acc = bank(n, [P, len(blocks), 2, P])
@@ -256,7 +256,7 @@ def tile_attend_gtwoemb_ln_kernel(tc, aT, bT, W, dz, gam, offs, soffs, out_0, ou
                     mean[:, pair], neg_dev[:, pair], -1.0, neg_shift[:, pair], ALU.mult, ALU.subtract
                 )
                 nc.vector.reciprocal(inv_var_d[:, pair], var_d[:, pair])
-                nc.scalar.activation(rstd[:, pair], inv_var_d[:, pair], ACT.Sqrt)
+                nc.scalar.activation(rstd[:, pair], inv_var_d[:, pair], ACT.Sqrt, scale=root_d[:])
                 nc.vector.tensor_tensor(hc_mean[jp][:], hc[:, pair], mean[:, pair], ALU.mult)
                 nc.vector.scalar_tensor_tensor(slope[:, pair], hc[:, pair], -1.0, inv_var_d[:, pair], ALU.mult, ALU.mult)
                 for j in tiles:
@@ -276,7 +276,7 @@ def tile_attend_gtwoemb_ln_kernel(tc, aT, bT, W, dz, gam, offs, soffs, out_0, ou
                         var_d[:, col], dev_d[:, col], neg_dev[:, col], all_s2[:, col], ALU.mult, ALU.add
                     )
                 nc.vector.reciprocal(inv_var_d[:, pair], var_d[:, pair])
-                nc.scalar.activation(rstd[:, pair], inv_var_d[:, pair], ACT.Sqrt)
+                nc.scalar.activation(rstd[:, pair], inv_var_d[:, pair], ACT.Sqrt, scale=root_d[:])
                 nc.scalar.mul(neg_inv[:, pair], inv_var_d[:, pair], -1.0)
                 for j in tiles:
                     col = slice(j, j + 1)
@@ -297,12 +297,7 @@ def tile_attend_gtwoemb_ln_kernel(tc, aT, bT, W, dz, gam, offs, soffs, out_0, ou
             for jj in range(2):
                 j = 2 * jp + jj
                 turn(spread[:, jj, :], rstd[:, j : j + 1].to_broadcast([P, P]), True, True)
-            nc.scalar.activation(
-                rstd_rows[:, jp * HALF : (jp + 1) * HALF],
-                spread[:].rearrange("p a b -> p (a b)"),
-                ACT.Copy,
-                scale=root_d[:],
-            )
+            nc.scalar.copy(rstd_rows[:, jp * HALF : (jp + 1) * HALF], spread[:].rearrange("p a b -> p (a b)"))
 
         def finish_sum(jp, blocks, on_vector):
             cols = slice(blocks[0] * P, (blocks[-1] + 1) * P)
@@ -325,15 +320,34 @@ def tile_attend_gtwoemb_ln_kernel(tc, aT, bT, W, dz, gam, offs, soffs, out_0, ou
                 target = w_first[jp][:, blocks[0] : blocks[-1] + 1, :]
             nc.scalar.copy(target, acc[:].rearrange("p k a b -> p k (a b)"))
 
+        x_scale = stat("x_scale")
+        x_bias = stat("x_bias")
+
+        def finish_late(jp, n):
+            acc = bank(n, [P, 2, 2, P])
+            for jj in range(2):
+                j = 2 * jp + jj
+                col = slice(j, j + 1)
+                nc.scalar.activation(x_scale[:, col], slope[:, col], ACT.Copy, scale=rstd[:, col])
+                nc.scalar.activation(x_bias[:, col], offset[:, col], ACT.Copy, scale=rstd[:, col])
+                u_id = keep.tile([P, HALF], F32, name="u_late%d" % j)
+                v_id = keep.tile([P, HALF], F32, name="v_late%d" % j)
+                nc.scalar.activation(u_id[:], h_id[j][:, HALF:D], ACT.Copy, scale=rstd[:, col])
+                affine(v_id[:], x_id[j][:, HALF:D], x_scale[:, col], x_bias[:, col])
+                for n_term, term in enumerate((u_id, v_id)):
+                    for kk in range(2):
+                        turn(acc[:, kk, jj, :], term[:, rows(kk)], jj + n_term + kk == 0, jj + n_term + kk == 3)
+            nc.scalar.copy(w_second[:, :, jp * HALF : (jp + 1) * HALF], acc[:].rearrange("p k a b -> p k (a b)"))
+
         finish_stats(0)
         spread_rstd(0)
         finish_sum(0, (0,), True)
         finish_sum(0, (1,), False)
-        finish_sum(0, (2, 3), False)
         finish_stats(1)
         spread_rstd(1)
         finish_sum(1, (0, 1), False)
-        finish_sum(1, (2, 3), False)
+        finish_late(0, 3)
+        finish_late(1, 6)
 
         for jp in range(2):
             part = slice(jp * 16, (jp + 1) * 16)
@@ -346,7 +360,7 @@ def tile_attend_gtwoemb_ln_kernel(tc, aT, bT, W, dz, gam, offs, soffs, out_0, ou
                 if jp == 1:
                     nc.sync.dma_start(out=out_1[rows(k), :], in_=seg_win[k][:])
         for k in range(2, NB):
-            nc.vector.tensor_tensor(tok_win[k % 3][:].indirect(tok_list[:]), w_second[:, k - 2, :], rstd_rows[:], ALU.mult)
+            nc.vector.tensor_copy(tok_win[k % 3][:].indirect(tok_list[:]), w_second[:, k - 2, :])
             nc.sync.dma_start(out=out_0[rows(k), :], in_=tok_win[k % 3][:])
-            nc.vector.tensor_tensor(seg_win[k % 2][:].indirect(seg_list[:]), w_second[:, k - 2, :], rstd_rows[:], ALU.mult)
+            nc.vector.tensor_copy(seg_win[k % 2][:].indirect(seg_list[:]), w_second[:, k - 2, :])
             nc.sync.dma_start(out=out_1[rows(k), :], in_=seg_win[k % 2][:])

from contextlib import ExitStack

import concourse.mybir as mybir
from concourse.masks import make_identity

F32 = mybir.dt.float32
BF16 = mybir.dt.bfloat16
U32 = mybir.dt.uint32
I32 = mybir.dt.int32
U16 = mybir.dt.uint16
U8 = mybir.dt.uint8
E4M3 = mybir.dt.float8_e4m3fn_x4
E5M2 = mybir.dt.float8_e5m2_x4
ALU = mybir.AluOpType
ACT = mybir.ActivationFunctionType

P = 128
D = 512
SLOTS = 512
TOKENS = 2048
SEGMENTS = 1024
NB = 4
HALF = 256
VECTOR_COLS = 336
FLOPS = 2 * 512 * 512 * 512


def tile_attend_gtwoemb_ln_kernel(tc, aT, bT, W, dz, gam, offs, soffs, out_0, out_1):
    nc = tc.nc
    with ExitStack() as ctx:
        keep = ctx.enter_context(tc.tile_pool(name="keep", bufs=1))
        spare = ctx.enter_context(tc.tile_pool(name="spare", bufs=4))
        psum = ctx.enter_context(tc.psum_pool(name="psum", bufs=1))

        def bank(n, shape):
            return psum.tile(shape, F32, name="bank", tag="bank%d" % n)

        def stat(name):
            return keep.tile([P, NB], F32, name=name)

        def rows(k):
            return slice(k * P, (k + 1) * P)

        def turn(out, in_, start, stop):
            nc.tensor.matmul(out, lhsT=in_, rhs=ident[:], start=start, stop=stop, is_transpose=True)

        tok_list = keep.tile([P, SLOTS // 16], U16, name="tok_list")
        seg_list = keep.tile([P, SLOTS // 16], U16, name="seg_list")
        dz_raw = keep.tile([P, 4, SLOTS], F32, name="dz_raw")
        w_raw = keep.tile([P, 4, D], F32, name="w_raw")
        a_tab = [keep.tile([P, TOKENS], F32, name="a_tab%d" % k) for k in range(NB)]
        b_tab = [keep.tile([P, SEGMENTS], F32, name="b_tab%d" % k) for k in range(NB)]
        gam_rows = keep.tile([P, P], F32, name="gam_rows")
        nc.sync.dma_start(out=gam_rows[:], in_=gam[0 : P // NB, :].rearrange("r (k c) -> (r k) c", k=NB))
        nc.sync.dma_start(out=w_raw[:], in_=W.rearrange("(p t) d -> p t d", t=4))
        nc.sync.dma_start(out=dz_raw[:], in_=dz.rearrange("(p t) i -> p t i", t=4))
        nc.sync.dma_start(tok_list[:], offs)
        nc.sync.dma_start(seg_list[:], soffs)
        for k in range(NB):
            nc.sync.dma_start(out=b_tab[k][:], in_=bT[rows(k), :])
            nc.sync.dma_start(out=a_tab[k][:], in_=aT[rows(k), :])

        ident = keep.tile([P, P], F32, name="ident")
        make_identity(nc, ident[:])

        count = keep.tile([P, 1], F32, name="count")
        root_d = keep.tile([P, 1], F32, name="root_d")
        nc.vector.memset(count[:], float(D * D))
        nc.scalar.activation(root_d[:], count[:], ACT.Sqrt)


        gam_ps = bank(7, [P, P])
        turn(gam_ps[:], gam_rows[:], True, True)
        gam_col = stat("gam_col")
        nc.scalar.copy(gam_col[:], gam_ps[:, 0:NB])
        gam_spread = bank(6, [P, D])
        for k in range(NB):
            turn(gam_spread[:, rows(k)], gam_col[:, k : k + 1].to_broadcast([P, P]), True, True)
        gam_all = keep.tile([P, D], F32, name="gam_all")
        nc.scalar.copy(gam_all[:], gam_spread[:])

        def quantise(raw, name, fmt, shares):
            woven = keep.tile([P, 512, 4], BF16, name=name + "_woven", align_bytes=64)
            codes = keep.tile([P, 512], U32, name=name + "_codes", align_bytes=64)
            scales = keep.tile([P, 512], U8, name=name + "_scales", align_bytes=64)
            for copy, cols in shares:
                copy(
                    out=woven[:, cols, :].rearrange("p (c i) t -> p c t i", i=4),
                    in_=raw[:, :, cols].rearrange("p t (c i) -> p c t i", i=4),
                )
            nc.vector.quantize_mx(
                out=codes[:].bitcast(fmt), scales=scales[:], in_=woven[:].rearrange("p c t -> p (c t)")
            )
            return codes, scales

        w_codes, w_scales = quantise(w_raw, "w", E4M3, [(nc.vector.tensor_copy, slice(0, D))])
        dz_codes, dz_scales = quantise(
            dz_raw, "dz", E5M2, [(nc.vector.tensor_copy, slice(0, VECTOR_COLS)), (nc.scalar.copy, slice(VECTOR_COLS, SLOTS))]
        )

        h_id = [keep.tile([P, D], F32, name="h_id%d" % j) for j in range(NB)]
        h1 = stat("h1")
        dn = [bank(j, [P, D]) for j in range(NB)]
        for j in range(NB):
            nc.tensor.matmul_mx(
                out=dn[j][:],
                lhsT=dz_codes[:, rows(j)].bitcast(E5M2),
                lhsT_scale=dz_scales[:, rows(j)],
                rhs=w_codes[:].bitcast(E4M3),
                rhs_scale=w_scales[:],
                start=True,
                stop=True,
            )
        a_got = [keep.tile([P, SLOTS], F32, name="a_got%d" % k) for k in range(NB)]
        b_got = [keep.tile([P, SLOTS], F32, name="b_got%d" % k) for k in range(NB)]
        x_id = [keep.tile([P, D], F32, name="x_id%d" % j) for j in range(NB)]
        s1 = [stat("s1_%d" % k) for k in range(NB)]
        s2 = [stat("s2_%d" % k) for k in range(3)]
        all_hx = stat("all_hx")
        neg_shift = stat("neg_shift")
        shift = stat("shift")

        def sum_x(k, j, src):
            nc.scalar.activation(x_id[j][:, rows(k)], src, ACT.Copy, accum_out=s1[k][:, j : j + 1])

        def sum_squares(k, j, width, src):
            squares = spare.tile([P, HALF], F32, name="squares")
            nc.scalar.activation(
                squares[:, 0:width], src, ACT.Square, bias=neg_shift[:, j : j + 1], accum_out=s2[k][:, j : j + 1]
            )

        def sum_hx(j, cols, total, products=None):
            if products is None:
                products = spare.tile([P, D], F32, name="products")
            nc.vector.scalar_tensor_tensor(
                products[:, cols],
                x_id[j][:, cols],
                neg_shift[:, j : j + 1],
                h_id[j][:, cols],
                ALU.add,
                ALU.mult,
                accum_out=total[:, j : j + 1],
            )

        for k in range(NB - 1):
            nc.vector.tensor_copy(b_got[k][:], b_tab[k][:].indirect(seg_list[:]))
            nc.vector.tensor_copy(a_got[k][:], a_tab[k][:].indirect(tok_list[:]))
            block = bank(4 + k % 2, [P, NB, P])
            for n, got in enumerate((b_got[k], a_got[k])):
                for j in range(NB):
                    turn(block[:, j, :], got[:, rows(j)], n == 0 and j == 0, n == 1 and j == NB - 1)
            for j in range(NB):
                sum_x(k, j, block[:, j, :])
            if k == 0:
                nc.scalar.mul(neg_shift[:], s1[0][:], -1.0 / P)
                nc.scalar.mul(shift[:], s1[0][:], 1.0 / P)
            if k < 2:
                for j in range(NB):
                    sum_squares(k, j, P, block[:, j, :])
        nc.vector.tensor_copy(b_got[3][:], b_tab[3][:].indirect(seg_list[:]))
        for jp in range(2):
            nc.vector.tensor_copy(
                a_got[3][:, jp * HALF : (jp + 1) * HALF], a_tab[3][:].indirect(tok_list[:, jp * 16 : (jp + 1) * 16])
            )

        for j in range(NB):
            nc.vector.scalar_tensor_tensor(
                h_id[j][:], dn[j][:], 1.0, gam_all[:], ALU.mult, ALU.mult, accum_out=h1[:, j : j + 1]
            )
        neg_h1n = stat("neg_h1n")
        nc.gpsimd.tensor_scalar(neg_h1n[:], h1[:], -1.0 / D, 0.0, ALU.mult, ALU.add)

        groups = [(0, (0,), 0), (0, (1,), 1), (1, (0, 1), 2)]
        sums = {}
        for jp, blocks, n in groups:
            acc = bank(n, [P, len(blocks), 2, P])
            sums[jp, blocks] = acc
            for kk, k in enumerate(blocks):
                for jj in range(2):
                    turn(acc[:, kk, jj, :], h_id[2 * jp + jj][:, rows(k)], kk + jj == 0, False)

        tok_win = [
            keep.tile([P, TOKENS], F32, name="tok_win0"),
            keep.tile([P, TOKENS], F32, name="tok_win1", tag="dz_woven", align_bytes=64),
            keep.tile([P, TOKENS], F32, name="tok_win2", tag="dz_codes", align_bytes=64),
        ]
        seg_win = [keep.tile([P, SEGMENTS], F32, name="seg_win%d" % n) for n in range(2)]
        for win in (tok_win[0], seg_win[0], seg_win[1]):
            nc.vector.memset(win[:].bitcast(I32), 0)
        for win in tok_win[1:]:
            nc.gpsimd.memset(win[:].bitcast(I32), 0)

        pair_s1 = stat("pair_s1")
        early_s1 = stat("early_s1")
        early_neg_dev = stat("early_neg_dev")
        early_s2 = stat("early_s2")
        first_s1 = stat("first_s1")
        nc.gpsimd.tensor_scalar(first_s1[:], s1[0][:], -3.0, 0.0, ALU.mult, ALU.add)
        nc.gpsimd.tensor_tensor(pair_s1[:], first_s1[:], s1[1][:], ALU.add)
        nc.gpsimd.tensor_tensor(early_s2[:], s2[0][:], s2[1][:], ALU.add)
        nc.gpsimd.tensor_tensor(early_s1[:], pair_s1[:], s1[2][:], ALU.add)
        nc.gpsimd.tensor_scalar(early_neg_dev[:], early_s1[:], -1.0 / D, 0.0, ALU.mult, ALU.add)

        dev_d = stat("dev_d")
        neg_dev = stat("neg_dev")
        all_s2 = stat("all_s2")
        var_d = stat("var_d")
        inv_var_d = stat("inv_var_d")
        hc = stat("hc")
        mean = stat("mean")
        hc_mean = [keep.tile([P, 2], F32, name="hc_mean%d" % jp) for jp in range(2)]
        slope = stat("slope")
        offset = stat("offset")
        rstd = stat("rstd")
        rstd_rows = keep.tile([P, SLOTS], F32, name="rstd_rows")
        w_first = [keep.tile([P, 2, HALF], F32, name="w_first%d" % jp) for jp in range(2)]
        w_second = keep.tile([P, 2, SLOTS], F32, name="w_second")

        neg_inv = stat("neg_inv")

        def affine(out, in_, scale, bias):
            nc.scalar.activation(out, in_, ACT.Identity, bias=bias, scale=scale)

        def finish_stats(jp):
            pair = slice(2 * jp, 2 * jp + 2)
            tiles = (2 * jp, 2 * jp + 1)
            last = bank((7, 5)[jp], [P, 2, P])
            for n, got in enumerate((b_got[3], a_got[3])):
                for j in tiles:
                    turn(last[:, j % 2, :], got[:, rows(j)], n == 0 and j % 2 == 0, n == 1 and j % 2 == 1)
            for j in tiles:
                sum_x(3, j, last[:, j % 2, :])
            for j in tiles:
                sum_squares(2, j, HALF, x_id[j][:, HALF:D])
            if jp == 1:
                held = keep.tile([P, 2, D], F32, name="held", tag="hc_mean0")
            for j in tiles:
                sum_hx(j, slice(0, D), all_hx, held[:, j % 2, :] if jp == 1 else None)
            if jp == 0:
                nc.vector.tensor_tensor(dev_d[:, pair], s1[3][:, pair], early_s1[:, pair], ALU.add)
                nc.vector.scalar_tensor_tensor(
                    neg_dev[:, pair], s1[3][:, pair], -1.0 / D, early_neg_dev[:, pair], ALU.mult, ALU.add
                )
                nc.vector.tensor_tensor(all_s2[:, pair], s2[2][:, pair], early_s2[:, pair], ALU.add)
                for j in tiles:
                    col = slice(j, j + 1)
                    nc.vector.scalar_tensor_tensor(
                        var_d[:, col], dev_d[:, col], neg_dev[:, col], all_s2[:, col], ALU.mult, ALU.add
                    )
                for j in tiles:
                    col = slice(j, j + 1)
                    nc.vector.scalar_tensor_tensor(
                        hc[:, col], h1[:, col], neg_dev[:, col], all_hx[:, col], ALU.mult, ALU.add
                    )
                nc.vector.scalar_tensor_tensor(
                    mean[:, pair], neg_dev[:, pair], -1.0, neg_shift[:, pair], ALU.mult, ALU.subtract
                )
                nc.vector.reciprocal(inv_var_d[:, pair], var_d[:, pair])
                nc.scalar.activation(rstd[:, pair], inv_var_d[:, pair], ACT.Sqrt, scale=root_d[:])
                nc.vector.tensor_tensor(hc_mean[jp][:], hc[:, pair], mean[:, pair], ALU.mult)
                nc.vector.scalar_tensor_tensor(slope[:, pair], hc[:, pair], -1.0, inv_var_d[:, pair], ALU.mult, ALU.mult)
                for j in tiles:
                    col = slice(j, j + 1)
                    nc.vector.scalar_tensor_tensor(
                        offset[:, col], hc_mean[jp][:, j % 2 : j % 2 + 1], inv_var_d[:, col], neg_h1n[:, col], ALU.mult, ALU.add
                    )
            else:
                nc.vector.tensor_tensor(dev_d[:, pair], s1[3][:, pair], early_s1[:, pair], ALU.add)
                nc.vector.scalar_tensor_tensor(
                    neg_dev[:, pair], s1[3][:, pair], -1.0 / D, early_neg_dev[:, pair], ALU.mult, ALU.add
                )
                nc.vector.tensor_tensor(all_s2[:, pair], s2[2][:, pair], early_s2[:, pair], ALU.add)
                for j in tiles:
                    col = slice(j, j + 1)
                    nc.vector.scalar_tensor_tensor(
                        var_d[:, col], dev_d[:, col], neg_dev[:, col], all_s2[:, col], ALU.mult, ALU.add
                    )
                nc.vector.reciprocal(inv_var_d[:, pair], var_d[:, pair])
                nc.scalar.activation(rstd[:, pair], inv_var_d[:, pair], ACT.Sqrt, scale=root_d[:])
                nc.scalar.mul(neg_inv[:, pair], inv_var_d[:, pair], -1.0)
                for j in tiles:
                    col = slice(j, j + 1)
                    affine(mean[:, col], neg_dev[:, col], -1.0, shift[:, col])
                    affine(hc[:, col], h1[:, col], neg_dev[:, col], all_hx[:, col])
                for j in tiles:
                    col = slice(j, j + 1)
                    nc.scalar.activation(hc_mean[jp][:, j % 2 : j % 2 + 1], hc[:, col], ACT.Copy, scale=mean[:, col])
                for j in tiles:
                    col = slice(j, j + 1)
                    nc.scalar.activation(slope[:, col], hc[:, col], ACT.Copy, scale=neg_inv[:, col])
                for j in tiles:
                    col = slice(j, j + 1)
                    affine(offset[:, col], hc_mean[jp][:, j % 2 : j % 2 + 1], inv_var_d[:, col], neg_h1n[:, col])

        def spread_rstd(jp):
            spread = bank((4, 0)[jp], [P, 2, P])
            for jj in range(2):
                j = 2 * jp + jj
                turn(spread[:, jj, :], rstd[:, j : j + 1].to_broadcast([P, P]), True, True)
            nc.scalar.copy(rstd_rows[:, jp * HALF : (jp + 1) * HALF], spread[:].rearrange("p a b -> p (a b)"))

        def finish_sum(jp, blocks, on_vector):
            cols = slice(blocks[0] * P, (blocks[-1] + 1) * P)
            v_id = {}
            for j in (2 * jp, 2 * jp + 1):
                v_id[j] = keep.tile([P, len(blocks), P], F32, name="v_id", tag="v_id%d_%d" % (j % 2, blocks[0]))
                col = slice(j, j + 1)
                flat = v_id[j][:].rearrange("p k c -> p (k c)")
                if on_vector:
                    nc.vector.tensor_scalar(flat, x_id[j][:, cols], slope[:, col], offset[:, col], ALU.mult, ALU.add)
                else:
                    affine(flat, x_id[j][:, cols], slope[:, col], offset[:, col])
            acc = sums[jp, blocks]
            for kk in range(len(blocks)):
                for jj in range(2):
                    turn(acc[:, kk, jj, :], v_id[2 * jp + jj][:, kk, :], False, kk == len(blocks) - 1 and jj == 1)
            if blocks[0] >= 2:
                target = w_second[:, :, jp * HALF : (jp + 1) * HALF]
            else:
                target = w_first[jp][:, blocks[0] : blocks[-1] + 1, :]
            nc.scalar.copy(target, acc[:].rearrange("p k a b -> p k (a b)"))

        x_scale = stat("x_scale")
        x_bias = stat("x_bias")

        def finish_late(jp, n):
            acc = bank(n, [P, 2, 2, P])
            for jj in range(2):
                j = 2 * jp + jj
                col = slice(j, j + 1)
                nc.scalar.activation(x_scale[:, col], slope[:, col], ACT.Copy, scale=rstd[:, col])
                nc.scalar.activation(x_bias[:, col], offset[:, col], ACT.Copy, scale=rstd[:, col])
                u_id = keep.tile([P, HALF], F32, name="u_late%d" % j)
                v_id = keep.tile([P, HALF], F32, name="v_late%d" % j)
                nc.scalar.activation(u_id[:], h_id[j][:, HALF:D], ACT.Copy, scale=rstd[:, col])
                affine(v_id[:], x_id[j][:, HALF:D], x_scale[:, col], x_bias[:, col])
                for n_term, term in enumerate((u_id, v_id)):
                    for kk in range(2):
                        turn(acc[:, kk, jj, :], term[:, rows(kk)], jj + n_term + kk == 0, jj + n_term + kk == 3)
            nc.scalar.copy(w_second[:, :, jp * HALF : (jp + 1) * HALF], acc[:].rearrange("p k a b -> p k (a b)"))

        finish_stats(0)
        spread_rstd(0)
        finish_sum(0, (0,), True)
        finish_sum(0, (1,), False)
        finish_stats(1)
        spread_rstd(1)
        finish_sum(1, (0, 1), False)
        finish_late(0, 3)
        finish_late(1, 6)

        for jp in range(2):
            part = slice(jp * 16, (jp + 1) * 16)
            factor = rstd_rows[:, jp * HALF : (jp + 1) * HALF]
            for k in range(2):
                nc.vector.tensor_tensor(tok_win[k][:].indirect(tok_list[:, part]), w_first[jp][:, k, :], factor, ALU.mult)
                if jp == 1:
                    nc.sync.dma_start(out=out_0[rows(k), :], in_=tok_win[k][:])
                nc.vector.tensor_tensor(seg_win[k][:].indirect(seg_list[:, part]), w_first[jp][:, k, :], factor, ALU.mult)
                if jp == 1:
                    nc.sync.dma_start(out=out_1[rows(k), :], in_=seg_win[k][:])
        for k in range(2, NB):
            nc.vector.tensor_copy(tok_win[k % 3][:].indirect(tok_list[:]), w_second[:, k - 2, :])
            nc.sync.dma_start(out=out_0[rows(k), :], in_=tok_win[k % 3][:])
            nc.vector.tensor_copy(seg_win[k % 2][:].indirect(seg_list[:]), w_second[:, k - 2, :])
            nc.sync.dma_start(out=out_1[rows(k), :], in_=seg_win[k % 2][:])
